import numpy as np
import ml_dtypes


def mxq(x, axis, fmt="e4m3"):
    dtype, down = {"e4m3": (ml_dtypes.float8_e4m3fn, 7), "e5m2": (ml_dtypes.float8_e5m2, 14)}[fmt]
    v = np.moveaxis(np.asarray(x, np.float32).astype(ml_dtypes.bfloat16).astype(np.float64), axis, -1)
    blocks = v.reshape(v.shape[:-1] + (-1, 32))
    amax = np.abs(blocks).max(-1, keepdims=True)
    byte = np.maximum(np.where(amax > 0, np.frexp(amax)[1] - 1 + 127, 0) - down, 1)
    scale = np.exp2(byte - 127.0)
    codes = (blocks / scale).astype(np.float32).astype(dtype).astype(np.float64)
    return np.moveaxis((codes * scale).reshape(v.shape), -1, axis)


WIDE = False


def mx_kscale(k):
    if not WIDE:
        return np.ones(k)
    levels = np.array([10, -10, 5, -5, 0])
    if k % 512:
        return np.exp2(np.random.permutation(np.resize(levels, k // 32))).repeat(32)
    a = np.empty((k // 512, 16))
    for p in range(k // 512):
        a[p, :8] = np.random.permutation(np.resize(levels, 8))
        for g in range(8):
            far = levels[np.abs(levels - a[p, g]) >= 10]
            a[p, g + 8] = far[np.random.randint(len(far))]
    return np.exp2(a.ravel()).repeat(32)


def f64(x):
    return np.asarray(x).astype(np.float64)


def striped(idx):
    return np.tile(idx.reshape(-1, 16).T, (8, 1)).astype(np.uint16)


def unstriped(offs):
    return offs[:16].T.reshape(-1).astype(np.int64)


def striped8(idx):
    return np.concatenate([v.reshape(-1, 16).T for v in idx]).astype(np.uint16)


def unstriped8(offs):
    return np.stack([offs[16 * g:16 * g + 16].T.reshape(-1) for g in range(8)]).astype(np.int64)


E2M1 = np.array([0.0, 0.5, 1.0, 1.5, 2.0, 3.0, 4.0, 6.0, -0.0, -0.5, -1.0, -1.5, -2.0, -3.0, -4.0, -6.0])


def pack_weight(w, fmt):
    k, n = w.shape
    w = f64(np.asarray(w, np.float32).astype(ml_dtypes.bfloat16)).reshape(k // 32, 32, n)
    amax = np.abs(w).max(1)
    if fmt == "e4m3":
        byte = np.frexp(amax)[1] - 1 + 127 - 7
    else:
        mant, ex = np.frexp(amax / 6.0)
        byte = np.where(mant > 0.5, ex, ex - 1) + 127
    byte = np.clip(np.where(amax > 0, byte, 1), 1, 254)
    scaled = (w * np.exp2(127.0 - byte)[:, None, :]).reshape(k, n).astype(np.float32)
    by_word = np.ascontiguousarray(scaled.reshape(k // 512, 128, 4, n).transpose(0, 1, 3, 2))
    if fmt == "e4m3":
        words = by_word.astype(ml_dtypes.float8_e4m3fn).view(np.uint8)
    else:
        c = by_word.astype(ml_dtypes.float4_e2m1fn).view(np.uint8) & 0xF
        words = (c[..., 0::2] | (c[..., 1::2] << 4)).reshape(k // 512, 128, 2 * n)
    return np.ascontiguousarray(words), np.ascontiguousarray(byte.astype(np.uint8).reshape(k // 512, 16, n))


def unpack_weight(words, scales, fmt):
    g, _, n = scales.shape
    words = np.ascontiguousarray(words).reshape(g, 128, n, -1)
    if fmt == "e4m3":
        vals = words.view(ml_dtypes.float8_e4m3fn).astype(np.float64)
    else:
        nib = np.empty((g, 128, n, 4), np.uint8)
        nib[..., 0::2] = words & 0xF
        nib[..., 1::2] = words >> 4
        vals = E2M1[nib]
    vals = vals * np.repeat(np.exp2(scales.astype(np.float64) - 127.0), 8, axis=1)[..., None]
    return vals.transpose(0, 1, 3, 2).reshape(g * 512, n)


def pack_table(v):
    words, scales = pack_weight(v, "e4m3")
    return np.concatenate([words.reshape(words.shape[0], -1), scales.reshape(scales.shape[0], -1)], axis=1)


def unpack_table(tab):
    g, t = tab.shape[0], tab.shape[1] // 528
    return unpack_weight(tab[:, :512 * t].reshape(g, 128, t, 4), tab[:, 512 * t:].reshape(g, 16, t), "e4m3")


K, M, T, S = 1536, 512, 1024, 512


def setup_inputs():
    n = np.random.standard_normal
    s = mx_kscale(K)[:, None]
    w = n((K, M)) / np.sqrt(K) / s
    p_w4 = pack_weight(w[512:], "e2m1")
    return {
        "tab": pack_table(n((K, T)) * s),
        "w8": (w[:512]).astype(np.float32),
        "w4_words": p_w4[0],
        "w4_scales": p_w4[1],
        "wgo": np.repeat(np.random.uniform(0.5, 2.0, (8, S)), 16, axis=0).astype(np.float32),
        "offs": striped(np.random.permutation(T)[:S]),
        "offs2": striped8(np.stack([np.random.permutation(T)[:S] for _ in range(8)])),
    }


def reference(tab, w8, w4_words, w4_scales, wgo, offs, offs2):
    tab_ = unpack_table(tab)[:, unstriped(offs)]
    w8_ = mxq(f64(w8), 0, "e4m3")
    w4_ = unpack_weight(w4_words, w4_scales, "e2m1")
    y = w8_.T @ tab_[:512] + w4_.T @ tab_[512:]
    place = unstriped8(offs2)[np.arange(M) % 128 // 16]
    out = np.zeros((M, T))
    out[np.arange(M)[:, None], place] = f64(wgo)[np.arange(M) % 128] * (y)
    return out

@@ -1,0 +1,151 @@
+from contextlib import ExitStack
+
+import concourse.mybir as mybir
+
+K, M, T, S = 1536, 512, 1024, 512
+FLOPS = 2 * K * M * S
+
+F32 = mybir.dt.float32
+BF16 = mybir.dt.bfloat16
+I32 = mybir.dt.int32
+U32 = mybir.dt.uint32
+U16 = mybir.dt.uint16
+U8 = mybir.dt.uint8
+FP8X4 = mybir.dt.float8_e4m3fn_x4
+FP4X4 = mybir.dt.float4_e2m1fn_x4
+MULT = mybir.AluOpType.mult
+
+P = 128
+PAGES = M // P
+HALF = S // 2
+WORD_BYTES = 512 * T
+
+
+def tile_list_tabhs_o_none_kernel(tc, tab, w8, w4_words, w4_scales, wgo, offs, offs2, out):
+    nc = tc.nc
+    with ExitStack() as ctx:
+        keep = ctx.enter_context(tc.tile_pool(name="keep", bufs=1))
+        psum = ctx.enter_context(tc.psum_pool(name="psum", bufs=1))
+
+        pick = keep.tile([P, S // 16], U16, name="pick")
+        place = keep.tile([P, S // 16], U16, name="place")
+        tab_scales = keep.tile([P, 2 * T], U8, name="tab_scales", align_bytes=64)
+        w4_planes = keep.tile([P, 2 * M], U8, name="w4_planes", align_bytes=64)
+        tab_words = [keep.tile([P, T], I32, name="tab_words%d" % a, align_bytes=64) for a in range(3)]
+        w4_codes = keep.tile([P, 2, 2 * M], U8, name="w4_codes", align_bytes=64)
+        gain = keep.tile([P, S], F32, name="gain", align_bytes=64)
+        pages = [keep.tile([P, T], F32, name="page%d" % m, align_bytes=64) for m in range(PAGES)]
+        w8_cols = [(0, P), (P, 2 * P), (2 * P, M)]
+        w8_raw = [keep.tile([P, 4, b - a], F32, name="w8_raw%d" % a, align_bytes=64) for a, b in w8_cols]
+
+        nc.vector.memset(tab_scales[:].bitcast(I32), 0)
+        nc.vector.memset(w4_planes[:].bitcast(I32), 0)
+        for m in range(PAGES):
+            nc.vector.memset(pages[m][:], 0.0)
+
+        def load_words(a):
+            src = tab[a, 0:WORD_BYTES].rearrange("(p b) -> p b", p=P)
+            nc.sync.dma_start(out=tab_words[a][:], in_=src.bitcast(I32))
+
+        def load_w8(i):
+            a, b = w8_cols[i]
+            nc.sync.dma_start(out=w8_raw[i][:], in_=w8[:, a:b].rearrange("(p j) n -> p j n", j=4))
+
+        nc.sync.dma_start(pick[:], offs)
+        for q in range(4):
+            rows = tab[1:3, WORD_BYTES + 4 * T * q : WORD_BYTES + 4 * T * (q + 1)].rearrange("a (r t) -> r a t", r=4)
+            dst = tab_scales[32 * q : 32 * q + 4, :].rearrange("r (a t) -> r a t", a=2)
+            nc.sync.dma_start(out=dst.bitcast(I32), in_=rows.bitcast(I32))
+        load_words(0)
+        load_words(1)
+        load_w8(0)
+        for q in range(4):
+            rows = tab[0, WORD_BYTES + 4 * T * q : WORD_BYTES + 4 * T * (q + 1)].rearrange("(r t) -> r t", r=4)
+            nc.sync.dma_start(out=tab_scales[32 * q + 4 : 32 * q + 8, 0:T].bitcast(I32), in_=rows.bitcast(I32))
+        load_words(2)
+        for q in range(4):
+            rows = w4_scales[:, 4 * q : 4 * q + 4, :].rearrange("a r n -> r a n")
+            dst = w4_planes[32 * q : 32 * q + 4, :].rearrange("r (a n) -> r a n", a=2)
+            nc.sync.dma_start(out=dst.bitcast(I32), in_=rows.bitcast(I32))
+        nc.sync.dma_start(out=w4_codes[:].bitcast(I32), in_=w4_words.rearrange("a p b -> p a b").bitcast(I32))
+        nc.sync.dma_start(place[:], offs2)
+        nc.sync.dma_start(out=gain[:], in_=wgo)
+        load_w8(1)
+        load_w8(2)
+
+        got_words = [keep.tile([P, S], I32, name="got_words%d" % a, align_bytes=64) for a in range(3)]
+        got_s01 = keep.tile([P, S], U8, name="got_s01", align_bytes=64)
+        got_s2 = keep.tile([P, S], U8, name="got_s2", align_bytes=64)
+        w8_codes = keep.tile([P, M], I32, name="w8_codes", align_bytes=64)
+        w8_plane = keep.tile([P, M], U8, name="w8_plane", align_bytes=64)
+        grouped = [keep.tile([P, P, 4], BF16, name="grouped%d" % m, align_bytes=64) for m in range(PAGES)]
+
+        def cast(m):
+            i = min(m, 2)
+            c0 = m * P - w8_cols[i][0]
+            nc.scalar.copy(out=grouped[m][:], in_=w8_raw[i][:, :, c0 : c0 + P].rearrange("p j n -> p n j"))
+
+        def quantise(m):
+            cols = slice(m * P, (m + 1) * P)
+            nc.vector.quantize_mx(
+                out=w8_codes[:, cols].bitcast(FP8X4),
+                scales=w8_plane[:, cols],
+                in_=grouped[m][:].rearrange("p n j -> p (n j)"),
+            )
+
+        def gather_words(a, j0, j1):
+            nc.vector.tensor_copy(
+                got_words[a][:, j0:j1].bitcast(U32), tab_words[a][:].bitcast(U32).indirect(pick[:, j0 // 16 : j1 // 16])
+            )
+
+        def multiply(acc, m, j0, j1):
+            cols = slice(m * P, (m + 1) * P)
+            nc.tensor.matmul_mx(
+                out=acc[:, 0 : j1 - j0],
+                lhsT=w8_codes[:, cols].bitcast(FP8X4),
+                lhsT_scale=w8_plane[:, cols],
+                rhs=got_words[0][:, j0:j1].bitcast(FP8X4),
+                rhs_scale=got_s01[4:P, j0:j1],
+                start=True,
+                stop=False,
+            )
+            step = S if j1 - j0 == S else P
+            for a in (1, 2):
+                plane = got_s01 if a == 1 else got_s2
+                for j in range(j0, j1, step):
+                    nc.tensor.matmul_mx(
+                        out=acc[:, j - j0 : j - j0 + step],
+                        lhsT=w4_codes[:, a - 1, 2 * m * P : 2 * (m + 1) * P].bitcast(FP4X4),
+                        lhsT_scale=w4_planes[:, (a - 1) * M + m * P : (a - 1) * M + (m + 1) * P],
+                        rhs=got_words[a][:, j : j + step].bitcast(FP8X4),
+                        rhs_scale=plane[:, j : j + step],
+                        start=False,
+                        stop=(a == 2 and j + step == j1),
+                    )
+
+        def finish(m, j0, j1):
+            acc = psum.tile([P, S], F32, name="acc%d_%d" % (m, j0))
+            multiply(acc, m, j0, j1)
+            y = keep.tile([P, j1 - j0], F32, name="y%d_%d" % (m, j0), align_bytes=64)
+            nc.scalar.copy(out=y[:], in_=acc[:, 0 : j1 - j0])
+            nc.vector.tensor_tensor(
+                pages[m][:].indirect(place[:, j0 // 16 : j1 // 16]), y[:], gain[:, j0:j1], MULT
+            )
+
+        nc.vector.tensor_copy(got_s2[:], tab_scales[:, T : 2 * T].indirect(pick[:]))
+        gather_words(0, 0, S)
+        gather_words(1, 0, S)
+        cast(0)
+        quantise(0)
+        nc.vector.tensor_copy(got_s01[:], tab_scales[:, 0:T].indirect(pick[:]))
+        gather_words(2, 0, HALF)
+        gather_words(2, HALF, S)
+        for m in range(1, PAGES):
+            cast(m)
+            quantise(m)
+        finish(0, 0, HALF)
+        finish(0, HALF, S)
+        nc.sync.dma_start(out=out[0:P, :], in_=pages[0][:])
+        for m in range(1, PAGES):
+            finish(m, 0, S)
+            nc.sync.dma_start(out=out[m * P : (m + 1) * P, :], in_=pages[m][:])

@@ -27,125 +27,145 @@ def tile_list_tabhs_o_none_kernel(tc, tab, w8, w4_words, w4_scales, wgo, offs, o
         keep = ctx.enter_context(tc.tile_pool(name="keep", bufs=1))
         psum = ctx.enter_context(tc.psum_pool(name="psum", bufs=1))
 
+        def sbuf(shape, dtype, name, tag=None):
+            return keep.tile(shape, dtype, name=name, tag=tag or name, align_bytes=64)
+
         pick = keep.tile([P, S // 16], U16, name="pick")
         place = keep.tile([P, S // 16], U16, name="place")
-        tab_scales = keep.tile([P, 2 * T], U8, name="tab_scales", align_bytes=64)
-        w4_planes = keep.tile([P, 2 * M], U8, name="w4_planes", align_bytes=64)
-        tab_words = [keep.tile([P, T], I32, name="tab_words%d" % a, align_bytes=64) for a in range(3)]
-        w4_codes = keep.tile([P, 2, 2 * M], U8, name="w4_codes", align_bytes=64)
-        gain = keep.tile([P, S], F32, name="gain", align_bytes=64)
-        pages = [keep.tile([P, T], F32, name="page%d" % m, align_bytes=64) for m in range(PAGES)]
-        w8_cols = [(0, P), (P, 2 * P), (2 * P, M)]
-        w8_raw = [keep.tile([P, 4, b - a], F32, name="w8_raw%d" % a, align_bytes=64) for a, b in w8_cols]
+        tab_scales = sbuf([P, 2 * T], U8, "tab_scales")
+        w4_planes = sbuf([P, 2 * M], U8, "w4_planes")
+        tab_words = [sbuf([P, T], I32, "tab_words%d" % a) for a in range(3)]
+        w4_codes = sbuf([P, 2, 2 * M], U8, "w4_codes")
+        gain = sbuf([P, S], F32, "gain")
+        pages = [sbuf([P, T], F32, "page%d" % m) for m in range(2)]
+        w8_raw = [sbuf([P, 4, 2 * P], F32, "w8_raw%d" % h) for h in range(2)]
 
         nc.vector.memset(tab_scales[:].bitcast(I32), 0)
         nc.vector.memset(w4_planes[:].bitcast(I32), 0)
-        for m in range(PAGES):
+        for m in range(2):
             nc.vector.memset(pages[m][:], 0.0)
 
         def load_words(a):
             src = tab[a, 0:WORD_BYTES].rearrange("(p b) -> p b", p=P)
             nc.sync.dma_start(out=tab_words[a][:], in_=src.bitcast(I32))
 
-        def load_w8(i):
-            a, b = w8_cols[i]
-            nc.sync.dma_start(out=w8_raw[i][:], in_=w8[:, a:b].rearrange("(p j) n -> p j n", j=4))
+        def load_w8(h):
+            src = w8[:, 2 * P * h : 2 * P * (h + 1)].rearrange("(p j) n -> p j n", j=4)
+            nc.sync.dma_start(out=w8_raw[h][:], in_=src)
 
         nc.sync.dma_start(pick[:], offs)
+        load_words(2)
         for q in range(4):
             rows = tab[1:3, WORD_BYTES + 4 * T * q : WORD_BYTES + 4 * T * (q + 1)].rearrange("a (r t) -> r a t", r=4)
             dst = tab_scales[32 * q : 32 * q + 4, :].rearrange("r (a t) -> r a t", a=2)
             nc.sync.dma_start(out=dst.bitcast(I32), in_=rows.bitcast(I32))
-        load_words(0)
         load_words(1)
-        load_w8(0)
+        load_words(0)
         for q in range(4):
             rows = tab[0, WORD_BYTES + 4 * T * q : WORD_BYTES + 4 * T * (q + 1)].rearrange("(r t) -> r t", r=4)
             nc.sync.dma_start(out=tab_scales[32 * q + 4 : 32 * q + 8, 0:T].bitcast(I32), in_=rows.bitcast(I32))
-        load_words(2)
+        load_w8(0)
+        nc.sync.dma_start(out=w4_codes[:].bitcast(I32), in_=w4_words.rearrange("a p b -> p a b").bitcast(I32))
         for q in range(4):
             rows = w4_scales[:, 4 * q : 4 * q + 4, :].rearrange("a r n -> r a n")
             dst = w4_planes[32 * q : 32 * q + 4, :].rearrange("r (a n) -> r a n", a=2)
             nc.sync.dma_start(out=dst.bitcast(I32), in_=rows.bitcast(I32))
-        nc.sync.dma_start(out=w4_codes[:].bitcast(I32), in_=w4_words.rearrange("a p b -> p a b").bitcast(I32))
         nc.sync.dma_start(place[:], offs2)
         nc.sync.dma_start(out=gain[:], in_=wgo)
         load_w8(1)
-        load_w8(2)
 
-        got_words = [keep.tile([P, S], I32, name="got_words%d" % a, align_bytes=64) for a in range(3)]
-        got_s01 = keep.tile([P, S], U8, name="got_s01", align_bytes=64)
-        got_s2 = keep.tile([P, S], U8, name="got_s2", align_bytes=64)
-        w8_codes = keep.tile([P, M], I32, name="w8_codes", align_bytes=64)
-        w8_plane = keep.tile([P, M], U8, name="w8_plane", align_bytes=64)
-        grouped = [keep.tile([P, P, 4], BF16, name="grouped%d" % m, align_bytes=64) for m in range(PAGES)]
+        w8_codes = sbuf([P, M], I32, "w8_codes")
+        w8_plane = sbuf([P, M], U8, "w8_plane")
 
-        def cast(m):
-            i = min(m, 2)
-            c0 = m * P - w8_cols[i][0]
-            nc.scalar.copy(out=grouped[m][:], in_=w8_raw[i][:, :, c0 : c0 + P].rearrange("p j n -> p n j"))
+        def cast(c0, c1):
+            h, first = divmod(c0, 2 * P)
+            grouped = sbuf([P, c1 - c0, 4], BF16, "grouped%d" % c0)
+            nc.scalar.copy(
+                out=grouped[:].rearrange("p (c i) j -> p c j i", i=4),
+                in_=w8_raw[h][:, :, first : first + c1 - c0].rearrange("p j (c i) -> p c j i", i=4),
+            )
+            return grouped
 
-        def quantise(m):
-            cols = slice(m * P, (m + 1) * P)
+        def quantise(grouped, c0, c1):
             nc.vector.quantize_mx(
-                out=w8_codes[:, cols].bitcast(FP8X4),
-                scales=w8_plane[:, cols],
-                in_=grouped[m][:].rearrange("p n j -> p (n j)"),
+                out=w8_codes[:, c0:c1].bitcast(FP8X4),
+                scales=w8_plane[:, c0:c1],
+                in_=grouped[:].rearrange("p n j -> p (n j)"),
             )
 
-        def gather_words(a, j0, j1):
-            nc.vector.tensor_copy(
-                got_words[a][:, j0:j1].bitcast(U32), tab_words[a][:].bitcast(U32).indirect(pick[:, j0 // 16 : j1 // 16])
-            )
+        def gather_words(dst, a, j0, j1):
+            window = tab_words[a][:].bitcast(U32)
+            nc.vector.tensor_copy(dst.bitcast(U32), window.indirect(pick[:, j0 // 16 : j1 // 16]))
 
-        def multiply(acc, m, j0, j1):
-            cols = slice(m * P, (m + 1) * P)
+        def gather_scales(dst, block, j0, j1):
+            window = tab_scales[:, block * T : (block + 1) * T]
+            nc.vector.tensor_copy(dst, window.indirect(pick[:, j0 // 16 : j1 // 16]))
+
+        got_w2 = sbuf([P, S], I32, "got_w2")
+        got_w1 = sbuf([P, S], I32, "got_w1")
+        got_s2 = sbuf([P, S], U8, "got_s2")
+        got_w0 = [sbuf([P, HALF], I32, "got_w0a")]
+        got_s01 = [sbuf([P, HALF], U8, "got_s01a")]
+
+        gather_words(got_w2[:], 2, 0, S)
+        gather_scales(got_s2[:], 1, 0, S)
+        gather_words(got_w1[:], 1, 0, S)
+        gather_words(got_w0[0][:], 0, 0, HALF)
+        gather_scales(got_s01[0][:], 0, 0, HALF)
+        grouped0 = cast(0, P)
+        quantise(grouped0, 0, P)
+        grouped1 = cast(P, 2 * P)
+        got_w0.append(sbuf([P, HALF], I32, "got_w0b", tag="w8_raw0"))
+        got_s01.append(sbuf([P, HALF], U8, "got_s01b", tag="grouped0"))
+        gather_words(got_w0[1][:], 0, HALF, S)
+        gather_scales(got_s01[1][:], 0, HALF, S)
+        quantise(grouped1, P, 2 * P)
+
+        def mx_pass(acc, m, a, j0, j1, first, start, stop):
+            h, i0 = divmod(j0, HALF)
+            i1 = i0 + j1 - j0
+            if a == 0:
+                lhs = w8_codes[:, m * P : (m + 1) * P].bitcast(FP8X4)
+                lhs_scale = w8_plane[:, m * P : (m + 1) * P]
+                rhs, rhs_scale = got_w0[h][:, i0:i1], got_s01[h][4:P, i0:i1]
+            else:
+                lhs = w4_codes[:, a - 1, 2 * m * P : 2 * (m + 1) * P].bitcast(FP4X4)
+                lhs_scale = w4_planes[:, (a - 1) * M + m * P : (a - 1) * M + (m + 1) * P]
+                if a == 1:
+                    rhs, rhs_scale = got_w1[:, j0:j1], got_s01[h][:, i0:i1]
+                else:
+                    rhs, rhs_scale = got_w2[:, j0:j1], got_s2[:, j0:j1]
             nc.tensor.matmul_mx(
-                out=acc[:, 0 : j1 - j0],
-                lhsT=w8_codes[:, cols].bitcast(FP8X4),
-                lhsT_scale=w8_plane[:, cols],
-                rhs=got_words[0][:, j0:j1].bitcast(FP8X4),
-                rhs_scale=got_s01[4:P, j0:j1],
-                start=True,
-                stop=False,
+                out=acc[:, j0 - first : j1 - first],
+                lhsT=lhs,
+                lhsT_scale=lhs_scale,
+                rhs=rhs.bitcast(FP8X4),
+                rhs_scale=rhs_scale,
+                start=start,
+                stop=stop,
             )
-            step = S if j1 - j0 == S else P
-            for a in (1, 2):
-                plane = got_s01 if a == 1 else got_s2
-                for j in range(j0, j1, step):
-                    nc.tensor.matmul_mx(
-                        out=acc[:, j - j0 : j - j0 + step],
-                        lhsT=w4_codes[:, a - 1, 2 * m * P : 2 * (m + 1) * P].bitcast(FP4X4),
-                        lhsT_scale=w4_planes[:, (a - 1) * M + m * P : (a - 1) * M + (m + 1) * P],
-                        rhs=got_words[a][:, j : j + step].bitcast(FP8X4),
-                        rhs_scale=plane[:, j : j + step],
-                        start=False,
-                        stop=(a == 2 and j + step == j1),
-                    )
 
-        def finish(m, j0, j1):
-            acc = psum.tile([P, S], F32, name="acc%d_%d" % (m, j0))
-            multiply(acc, m, j0, j1)
-            y = keep.tile([P, j1 - j0], F32, name="y%d_%d" % (m, j0), align_bytes=64)
+        def finish(m, j0, j1, bank, y_tag):
+            acc = psum.tile([P, S], F32, name="acc%d_%d" % (m, j0), tag=bank)
+            widths = {2: S if j1 - j0 == S else P, 1: P, 0: HALF}
+            for a in (2, 1, 0):
+                for j in range(j0, j1, widths[a]):
+                    mx_pass(acc, m, a, j, j + widths[a], j0, a == 2 and j == j0, a == 0 and j + widths[a] == j1)
+            y = sbuf([P, j1 - j0], F32, "y%d_%d" % (m, j0), tag=y_tag)
             nc.scalar.copy(out=y[:], in_=acc[:, 0 : j1 - j0])
             nc.vector.tensor_tensor(
                 pages[m][:].indirect(place[:, j0 // 16 : j1 // 16]), y[:], gain[:, j0:j1], MULT
             )
 
-        nc.vector.tensor_copy(got_s2[:], tab_scales[:, T : 2 * T].indirect(pick[:]))
-        gather_words(0, 0, S)
-        gather_words(1, 0, S)
-        cast(0)
-        quantise(0)
-        nc.vector.tensor_copy(got_s01[:], tab_scales[:, 0:T].indirect(pick[:]))
-        gather_words(2, 0, HALF)
-        gather_words(2, HALF, S)
-        for m in range(1, PAGES):
-            cast(m)
-            quantise(m)
-        finish(0, 0, HALF)
-        finish(0, HALF, S)
+        finish(0, 0, HALF, "bank0", None)
+        grouped2 = cast(2 * P, M)
+        quantise(grouped2, 2 * P, M)
+        for m, tag in ((2, "tab_words0"), (3, "grouped256")):
+            page = sbuf([P, T], F32, "page%d" % m, tag=tag)
+            nc.gpsimd.memset(page[:], 0.0)
+            pages.append(page)
+        finish(0, HALF, S, "bank1", None)
         nc.sync.dma_start(out=out[0:P, :], in_=pages[0][:])
         for m in range(1, PAGES):
-            finish(m, 0, S)
+            finish(m, 0, S, "bank%d" % ((m + 1) % 2), "w8_raw1" if m == 1 else None)
             nc.sync.dma_start(out=out[m * P : (m + 1) * P, :], in_=pages[m][:])

@@ -37,21 +37,22 @@ def tile_list_tabhs_o_none_kernel(tc, tab, w8, w4_words, w4_scales, wgo, offs, o
         tab_words = [sbuf([P, T], I32, "tab_words%d" % a) for a in range(3)]
         w4_codes = sbuf([P, 2, 2 * M], U8, "w4_codes")
         gain = sbuf([P, S], F32, "gain")
-        pages = [sbuf([P, T], F32, "page%d" % m) for m in range(2)]
-        w8_raw = [sbuf([P, 4, 2 * P], F32, "w8_raw%d" % h) for h in range(2)]
+        pages = [sbuf([P, T], F32, "page%d" % m) for m in range(PAGES)]
+        w8_cols = [(0, P), (P, 2 * P), (2 * P, M)]
+        w8_raw = [sbuf([P, 4, c1 - c0], F32, "w8_raw%d" % i) for i, (c0, c1) in enumerate(w8_cols)]
 
         nc.vector.memset(tab_scales[:].bitcast(I32), 0)
         nc.vector.memset(w4_planes[:].bitcast(I32), 0)
-        for m in range(2):
+        for m in range(PAGES):
             nc.vector.memset(pages[m][:], 0.0)
 
         def load_words(a):
             src = tab[a, 0:WORD_BYTES].rearrange("(p b) -> p b", p=P)
             nc.sync.dma_start(out=tab_words[a][:], in_=src.bitcast(I32))
 
-        def load_w8(h):
-            src = w8[:, 2 * P * h : 2 * P * (h + 1)].rearrange("(p j) n -> p j n", j=4)
-            nc.sync.dma_start(out=w8_raw[h][:], in_=src)
+        def load_w8(i):
+            c0, c1 = w8_cols[i]
+            nc.sync.dma_start(out=w8_raw[i][:], in_=w8[:, c0:c1].rearrange("(p j) n -> p j n", j=4))
 
         nc.sync.dma_start(pick[:], offs)
         load_words(2)
@@ -73,20 +74,22 @@ def tile_list_tabhs_o_none_kernel(tc, tab, w8, w4_words, w4_scales, wgo, offs, o
         nc.sync.dma_start(place[:], offs2)
         nc.sync.dma_start(out=gain[:], in_=wgo)
         load_w8(1)
+        load_w8(2)
 
         w8_codes = sbuf([P, M], I32, "w8_codes")
         w8_plane = sbuf([P, M], U8, "w8_plane")
 
-        def cast(c0, c1):
-            h, first = divmod(c0, 2 * P)
-            grouped = sbuf([P, c1 - c0, 4], BF16, "grouped%d" % c0)
+        def cast(i):
+            c0, c1 = w8_cols[i]
+            grouped = sbuf([P, c1 - c0, 4], BF16, "grouped%d" % i)
             nc.scalar.copy(
                 out=grouped[:].rearrange("p (c i) j -> p c j i", i=4),
-                in_=w8_raw[h][:, :, first : first + c1 - c0].rearrange("p j (c i) -> p c j i", i=4),
+                in_=w8_raw[i][:].rearrange("p j (c i) -> p c j i", i=4),
             )
             return grouped
 
-        def quantise(grouped, c0, c1):
+        def quantise(grouped, i):
+            c0, c1 = w8_cols[i]
             nc.vector.quantize_mx(
                 out=w8_codes[:, c0:c1].bitcast(FP8X4),
                 scales=w8_plane[:, c0:c1],
@@ -112,14 +115,11 @@ def tile_list_tabhs_o_none_kernel(tc, tab, w8, w4_words, w4_scales, wgo, offs, o
         gather_words(got_w1[:], 1, 0, S)
         gather_words(got_w0[0][:], 0, 0, HALF)
         gather_scales(got_s01[0][:], 0, 0, HALF)
-        grouped0 = cast(0, P)
-        quantise(grouped0, 0, P)
-        grouped1 = cast(P, 2 * P)
+        quantise(cast(0), 0)
         got_w0.append(sbuf([P, HALF], I32, "got_w0b", tag="w8_raw0"))
         got_s01.append(sbuf([P, HALF], U8, "got_s01b", tag="grouped0"))
         gather_words(got_w0[1][:], 0, HALF, S)
         gather_scales(got_s01[1][:], 0, HALF, S)
-        quantise(grouped1, P, 2 * P)
 
         def mx_pass(acc, m, a, j0, j1, first, start, stop):
             h, i0 = divmod(j0, HALF)
@@ -158,14 +158,10 @@ def tile_list_tabhs_o_none_kernel(tc, tab, w8, w4_words, w4_scales, wgo, offs, o
             )
 
         finish(0, 0, HALF, "bank0", None)
-        grouped2 = cast(2 * P, M)
-        quantise(grouped2, 2 * P, M)
-        for m, tag in ((2, "tab_words0"), (3, "grouped256")):
-            page = sbuf([P, T], F32, "page%d" % m, tag=tag)
-            nc.gpsimd.memset(page[:], 0.0)
-            pages.append(page)
-        finish(0, HALF, S, "bank1", None)
+        quantise(cast(1), 1)
+        finish(0, HALF, S, "bank1", "w8_raw1")
         nc.sync.dma_start(out=out[0:P, :], in_=pages[0][:])
+        quantise(cast(2), 2)
         for m in range(1, PAGES):
-            finish(m, 0, S, "bank%d" % ((m + 1) % 2), "w8_raw1" if m == 1 else None)
+            finish(m, 0, S, "bank%d" % ((m + 1) % 2), "w8_raw2" if m == 1 else None)
             nc.sync.dma_start(out=out[m * P : (m + 1) * P, :], in_=pages[m][:])

@@ -37,14 +37,14 @@ def tile_list_tabhs_o_none_kernel(tc, tab, w8, w4_words, w4_scales, wgo, offs, o
         tab_words = [sbuf([P, T], I32, "tab_words%d" % a) for a in range(3)]
         w4_codes = sbuf([P, 2, 2 * M], U8, "w4_codes")
         gain = sbuf([P, S], F32, "gain")
-        pages = [sbuf([P, T], F32, "page%d" % m) for m in range(PAGES)]
+        pages = [sbuf([P, T], F32, "page%d" % m) for m in range(PAGES - 1)]
         w8_cols = [(0, P), (P, 2 * P), (2 * P, M)]
         w8_raw = [sbuf([P, 4, c1 - c0], F32, "w8_raw%d" % i) for i, (c0, c1) in enumerate(w8_cols)]
 
         nc.vector.memset(tab_scales[:].bitcast(I32), 0)
         nc.vector.memset(w4_planes[:].bitcast(I32), 0)
-        for m in range(PAGES):
-            nc.vector.memset(pages[m][:], 0.0)
+        for page in pages:
+            nc.vector.memset(page[:], 0.0)
 
         def load_words(a):
             src = tab[a, 0:WORD_BYTES].rearrange("(p b) -> p b", p=P)
@@ -54,8 +54,8 @@ def tile_list_tabhs_o_none_kernel(tc, tab, w8, w4_words, w4_scales, wgo, offs, o
             c0, c1 = w8_cols[i]
             nc.sync.dma_start(out=w8_raw[i][:], in_=w8[:, c0:c1].rearrange("(p j) n -> p j n", j=4))
 
-        nc.sync.dma_start(pick[:], offs)
         load_words(2)
+        nc.sync.dma_start(pick[:], offs)
         for q in range(4):
             rows = tab[1:3, WORD_BYTES + 4 * T * q : WORD_BYTES + 4 * T * (q + 1)].rearrange("a (r t) -> r a t", r=4)
             dst = tab_scales[32 * q : 32 * q + 4, :].rearrange("r (a t) -> r a t", a=2)
@@ -162,6 +162,8 @@ def tile_list_tabhs_o_none_kernel(tc, tab, w8, w4_words, w4_scales, wgo, offs, o
         finish(0, HALF, S, "bank1", "w8_raw1")
         nc.sync.dma_start(out=out[0:P, :], in_=pages[0][:])
         quantise(cast(2), 2)
+        pages.append(sbuf([P, T], F32, "page3", tag="grouped2"))
+        nc.gpsimd.memset(pages[3][:], 0.0)
         for m in range(1, PAGES):
             finish(m, 0, S, "bank%d" % ((m + 1) % 2), "w8_raw2" if m == 1 else None)
             nc.sync.dma_start(out=out[m * P : (m + 1) * P, :], in_=pages[m][:])

from contextlib import ExitStack

import concourse.mybir as mybir

K, M, T, S = 1536, 512, 1024, 512
FLOPS = 2 * K * M * S

F32 = mybir.dt.float32
BF16 = mybir.dt.bfloat16
I32 = mybir.dt.int32
U32 = mybir.dt.uint32
U16 = mybir.dt.uint16
U8 = mybir.dt.uint8
FP8X4 = mybir.dt.float8_e4m3fn_x4
FP4X4 = mybir.dt.float4_e2m1fn_x4
MULT = mybir.AluOpType.mult

P = 128
PAGES = M // P
HALF = S // 2
WORD_BYTES = 512 * T


def tile_list_tabhs_o_none_kernel(tc, tab, w8, w4_words, w4_scales, wgo, offs, offs2, out):
    nc = tc.nc
    with ExitStack() as ctx:
        keep = ctx.enter_context(tc.tile_pool(name="keep", bufs=1))
        psum = ctx.enter_context(tc.psum_pool(name="psum", bufs=1))

        def sbuf(shape, dtype, name, tag=None):
            return keep.tile(shape, dtype, name=name, tag=tag or name, align_bytes=64)

        pick = keep.tile([P, S // 16], U16, name="pick")
        place = keep.tile([P, S // 16], U16, name="place")
        tab_scales = sbuf([P, 2 * T], U8, "tab_scales")
        w4_planes = sbuf([P, 2 * M], U8, "w4_planes")
        tab_words = [sbuf([P, T], I32, "tab_words%d" % a) for a in range(3)]
        w4_codes = sbuf([P, 2, 2 * M], U8, "w4_codes")
        gain = sbuf([P, S], F32, "gain")
        pages = [sbuf([P, T], F32, "page%d" % m) for m in range(PAGES - 1)]
        w8_cols = [(0, P), (P, 2 * P), (2 * P, M)]
        w8_raw = [sbuf([P, 4, c1 - c0], F32, "w8_raw%d" % i) for i, (c0, c1) in enumerate(w8_cols)]

        nc.vector.memset(tab_scales[:].bitcast(I32), 0)
        nc.vector.memset(w4_planes[:].bitcast(I32), 0)
        for page in pages:
            nc.vector.memset(page[:], 0.0)

        def load_words(a):
            src = tab[a, 0:WORD_BYTES].rearrange("(p b) -> p b", p=P)
            nc.sync.dma_start(out=tab_words[a][:], in_=src.bitcast(I32))

        def load_w8(i):
            c0, c1 = w8_cols[i]
            nc.sync.dma_start(out=w8_raw[i][:], in_=w8[:, c0:c1].rearrange("(p j) n -> p j n", j=4))

        load_words(2)
        nc.sync.dma_start(pick[:], offs)
        for q in range(4):
            rows = tab[1:3, WORD_BYTES + 4 * T * q : WORD_BYTES + 4 * T * (q + 1)].rearrange("a (r t) -> r a t", r=4)
            dst = tab_scales[32 * q : 32 * q + 4, :].rearrange("r (a t) -> r a t", a=2)
            nc.sync.dma_start(out=dst.bitcast(I32), in_=rows.bitcast(I32))
        load_words(1)
        load_words(0)
        for q in range(4):
            rows = tab[0, WORD_BYTES + 4 * T * q : WORD_BYTES + 4 * T * (q + 1)].rearrange("(r t) -> r t", r=4)
            nc.sync.dma_start(out=tab_scales[32 * q + 4 : 32 * q + 8, 0:T].bitcast(I32), in_=rows.bitcast(I32))
        load_w8(0)
        nc.sync.dma_start(out=w4_codes[:].bitcast(I32), in_=w4_words.rearrange("a p b -> p a b").bitcast(I32))
        for q in range(4):
            rows = w4_scales[:, 4 * q : 4 * q + 4, :].rearrange("a r n -> r a n")
            dst = w4_planes[32 * q : 32 * q + 4, :].rearrange("r (a n) -> r a n", a=2)
            nc.sync.dma_start(out=dst.bitcast(I32), in_=rows.bitcast(I32))
        nc.sync.dma_start(place[:], offs2)
        nc.sync.dma_start(out=gain[:], in_=wgo)
        load_w8(1)
        load_w8(2)

        w8_codes = sbuf([P, M], I32, "w8_codes")
        w8_plane = sbuf([P, M], U8, "w8_plane")

        def cast(i):
            c0, c1 = w8_cols[i]
            grouped = sbuf([P, c1 - c0, 4], BF16, "grouped%d" % i)
            nc.scalar.copy(
                out=grouped[:].rearrange("p (c i) j -> p c j i", i=4),
                in_=w8_raw[i][:].rearrange("p j (c i) -> p c j i", i=4),
            )
            return grouped

        def quantise(grouped, i):
            c0, c1 = w8_cols[i]
            nc.vector.quantize_mx(
                out=w8_codes[:, c0:c1].bitcast(FP8X4),
                scales=w8_plane[:, c0:c1],
                in_=grouped[:].rearrange("p n j -> p (n j)"),
            )

        def gather_words(dst, a, j0, j1):
            window = tab_words[a][:].bitcast(U32)
            nc.vector.tensor_copy(dst.bitcast(U32), window.indirect(pick[:, j0 // 16 : j1 // 16]))

        def gather_scales(dst, block, j0, j1):
            window = tab_scales[:, block * T : (block + 1) * T]
            nc.vector.tensor_copy(dst, window.indirect(pick[:, j0 // 16 : j1 // 16]))

        got_w2 = sbuf([P, S], I32, "got_w2")
        got_w1 = sbuf([P, S], I32, "got_w1")
        got_s2 = sbuf([P, S], U8, "got_s2")
        got_w0 = [sbuf([P, HALF], I32, "got_w0a")]
        got_s01 = [sbuf([P, HALF], U8, "got_s01a")]

        gather_words(got_w2[:], 2, 0, S)
        gather_scales(got_s2[:], 1, 0, S)
        gather_words(got_w1[:], 1, 0, S)
        gather_words(got_w0[0][:], 0, 0, HALF)
        gather_scales(got_s01[0][:], 0, 0, HALF)
        quantise(cast(0), 0)
        got_w0.append(sbuf([P, HALF], I32, "got_w0b", tag="w8_raw0"))
        got_s01.append(sbuf([P, HALF], U8, "got_s01b", tag="grouped0"))
        gather_words(got_w0[1][:], 0, HALF, S)
        gather_scales(got_s01[1][:], 0, HALF, S)

        def mx_pass(acc, m, a, j0, j1, first, start, stop):
            h, i0 = divmod(j0, HALF)
            i1 = i0 + j1 - j0
            if a == 0:
                lhs = w8_codes[:, m * P : (m + 1) * P].bitcast(FP8X4)
                lhs_scale = w8_plane[:, m * P : (m + 1) * P]
                rhs, rhs_scale = got_w0[h][:, i0:i1], got_s01[h][4:P, i0:i1]
            else:
                lhs = w4_codes[:, a - 1, 2 * m * P : 2 * (m + 1) * P].bitcast(FP4X4)
                lhs_scale = w4_planes[:, (a - 1) * M + m * P : (a - 1) * M + (m + 1) * P]
                if a == 1:
                    rhs, rhs_scale = got_w1[:, j0:j1], got_s01[h][:, i0:i1]
                else:
                    rhs, rhs_scale = got_w2[:, j0:j1], got_s2[:, j0:j1]
            nc.tensor.matmul_mx(
                out=acc[:, j0 - first : j1 - first],
                lhsT=lhs,
                lhsT_scale=lhs_scale,
                rhs=rhs.bitcast(FP8X4),
                rhs_scale=rhs_scale,
                start=start,
                stop=stop,
            )

        def finish(m, j0, j1, bank, y_tag):
            acc = psum.tile([P, S], F32, name="acc%d_%d" % (m, j0), tag=bank)
            widths = {2: S if j1 - j0 == S else P, 1: P, 0: HALF}
            for a in (2, 1, 0):
                for j in range(j0, j1, widths[a]):
                    mx_pass(acc, m, a, j, j + widths[a], j0, a == 2 and j == j0, a == 0 and j + widths[a] == j1)
            y = sbuf([P, j1 - j0], F32, "y%d_%d" % (m, j0), tag=y_tag)
            nc.scalar.copy(out=y[:], in_=acc[:, 0 : j1 - j0])
            nc.vector.tensor_tensor(
                pages[m][:].indirect(place[:, j0 // 16 : j1 // 16]), y[:], gain[:, j0:j1], MULT
            )

        finish(0, 0, HALF, "bank0", None)
        quantise(cast(1), 1)
        finish(0, HALF, S, "bank1", "w8_raw1")
        nc.sync.dma_start(out=out[0:P, :], in_=pages[0][:])
        quantise(cast(2), 2)
        pages.append(sbuf([P, T], F32, "page3", tag="grouped2"))
        nc.gpsimd.memset(pages[3][:], 0.0)
        for m in range(1, PAGES):
            finish(m, 0, S, "bank%d" % ((m + 1) % 2), "w8_raw2" if m == 1 else None)
            nc.sync.dma_start(out=out[m * P : (m + 1) * P, :], in_=pages[m][:])
